import numpy as np
import ml_dtypes


def mxq(x, axis, fmt="e4m3"):
    dtype, down = {"e4m3": (ml_dtypes.float8_e4m3fn, 7), "e5m2": (ml_dtypes.float8_e5m2, 14)}[fmt]
    v = np.moveaxis(np.asarray(x, np.float32).astype(ml_dtypes.bfloat16).astype(np.float64), axis, -1)
    blocks = v.reshape(v.shape[:-1] + (-1, 32))
    amax = np.abs(blocks).max(-1, keepdims=True)
    byte = np.maximum(np.where(amax > 0, np.frexp(amax)[1] - 1 + 127, 0) - down, 1)
    scale = np.exp2(byte - 127.0)
    codes = (blocks / scale).astype(np.float32).astype(dtype).astype(np.float64)
    return np.moveaxis((codes * scale).reshape(v.shape), -1, axis)


WIDE = False


def mx_kscale(k):
    if not WIDE:
        return np.ones(k)
    levels = np.array([10, -10, 5, -5, 0])
    if k % 512:
        return np.exp2(np.random.permutation(np.resize(levels, k // 32))).repeat(32)
    a = np.empty((k // 512, 16))
    for p in range(k // 512):
        a[p, :8] = np.random.permutation(np.resize(levels, 8))
        for g in range(8):
            far = levels[np.abs(levels - a[p, g]) >= 10]
            a[p, g + 8] = far[np.random.randint(len(far))]
    return np.exp2(a.ravel()).repeat(32)


def f64(x):
    return np.asarray(x).astype(np.float64)


def striped(idx):
    return np.tile(np.asarray(idx).reshape(-1, 16).T, (8, 1)).astype(np.uint16)


def unstriped(offs):
    return offs[:16].T.reshape(-1).astype(np.int64)


O, G, T, D, M = 3, 256, 1024, 1024, 256


def setup_inputs():
    n = np.random.standard_normal
    s = mx_kscale(D)[:, None]
    x = n((D, T)) * s
    x[:, 0] = 0.0
    idx = np.stack([np.random.permutation(T - 1)[:G] + 1 for o in range(O)])
    idx[np.random.uniform(size=(O, G)) < 0.1] = 0
    return {
        "xT": x.astype(np.float32),
        "w": (n((O, D, M)) / np.sqrt(O * D) / s).astype(np.float32),
        "bias": (0.3 * n((M, 1))).astype(np.float32),
        "offs": striped(idx.reshape(-1)),
    }


def reference(xT, w, bias, offs):
    x = f64(xT)[:, unstriped(offs)]
    wq, xq = mxq(f64(w), 1, "e4m3"), mxq(x, 0, "e4m3").reshape(D, O, G)
    y = sum(wq[o].T @ xq[:, o] for o in range(O))
    y = y + f64(bias)
    return y

@@ -1,0 +1,162 @@
+from contextlib import ExitStack
+
+import concourse.mybir as mybir
+
+RELS, SITES, COLS, D, M = 3, 256, 1024, 1024, 256
+FLOPS = 2 * RELS * SITES * D * M
+
+F32 = mybir.dt.float32
+BF16 = mybir.dt.bfloat16
+U32 = mybir.dt.uint32
+U16 = mybir.dt.uint16
+U8 = mybir.dt.uint8
+FP8X4 = mybir.dt.float8_e4m3fn_x4
+ADD = mybir.AluOpType.add
+MULT = mybir.AluOpType.mult
+COPY = mybir.ActivationFunctionType.Copy
+IDENTITY = mybir.ActivationFunctionType.Identity
+
+P = 128
+ENTRIES = RELS * SITES
+GATHERS = ((0, 384), (384, 768))
+PIECES = ((0, 512), (512, 768))
+
+
+def tile_attend_spconv_bias_kernel(tc, xT, w, bias, offs, out):
+    nc = tc.nc
+    with ExitStack() as ctx:
+        keep = ctx.enter_context(tc.tile_pool(name="keep", bufs=1))
+        psum = ctx.enter_context(tc.psum_pool(name="psum", bufs=1))
+
+        offsets = keep.tile([P, ENTRIES // 16], U16, name="offsets")
+        nc.sync.dma_start(offsets[:], offs)
+        bias_t = keep.tile([P, 2], F32, name="bias_t")
+        with nc.allow_non_contiguous_dma(reason="256 biases, one a partition and m tile"):
+            nc.scalar.dma_start(out=bias_t[:], in_=bias.rearrange("(t p) o -> p (t o)", p=P))
+
+        x_rows = xT.rearrange("(g p u e) c -> g u p e c", g=2, p=P, u=2, e=2)
+        w_rows = w.rearrange("o (g p j) m -> o g p j m", g=2, p=P, j=4)
+
+        x_raw = {}
+        for g in range(2):
+            for u in range(2):
+                x_raw[g, u] = keep.tile([P, 2, COLS], F32, name=f"x_raw{g}{u}")
+                halves = 2 if (g, u) == (0, 0) else 1
+                step = COLS // halves
+                for h in range(halves):
+                    cols = slice(h * step, (h + 1) * step)
+                    nc.sync.dma_start(out=x_raw[g, u][:, :, cols], in_=x_rows[g, u][:, :, cols])
+        w_raw = {}
+        for g in range(2):
+            for o in range(RELS):
+                w_raw[o, g] = keep.tile([P, 4, M], F32, name=f"w_raw{o}{g}")
+                nc.sync.dma_start(out=w_raw[o, g][:], in_=w_rows[o, g])
+
+        x_pairs, x_in, x_codes, x_scales = {}, {}, {}, {}
+        for g in range(2):
+            for u in range(2):
+                x_pairs[g, u] = keep.tile([P, COLS, 2], BF16, name=f"x_pairs{g}{u}", align_bytes=64)
+            x_in[g] = keep.tile([P, ENTRIES, 4], BF16, name=f"x_in{g}", align_bytes=64)
+            x_codes[g] = keep.tile([P, ENTRIES], U32, name=f"x_codes{g}", align_bytes=64)
+            x_scales[g] = keep.tile([P, ENTRIES], U8, name=f"x_scales{g}", align_bytes=64)
+        w_in, w_codes, w_scales = {}, {}, {}
+        for g in range(2):
+            for o in range(RELS):
+                w_in[o, g] = keep.tile([P, M, 4], BF16, name=f"w_in{o}{g}", align_bytes=64)
+                w_codes[o, g] = keep.tile([P, M], U32, name=f"w_codes{o}{g}", align_bytes=64)
+                w_scales[o, g] = keep.tile([P, M], U8, name=f"w_scales{o}{g}", align_bytes=64)
+
+        def cast(engine, dst, src):
+            if engine == "s":
+                nc.scalar.activation(out=dst, in_=src, func=COPY)
+            elif engine == "g":
+                nc.gpsimd.tensor_scalar(dst, src, 1.0, 0.0, MULT, ADD)
+            else:
+                nc.vector.tensor_copy(out=dst, in_=src)
+
+        def cast_x(g, u, parts):
+            a = 0
+            for engine, n in parts:
+                cols = slice(a, a + n)
+                cast(engine, x_pairs[g, u][:, cols, :], x_raw[g, u][:, :, cols].rearrange("p e c -> p c e"))
+                a += n
+
+        def cast_w(o, g, parts):
+            a = 0
+            for engine, n in parts:
+                cols = slice(a, a + n)
+                cast(engine, w_in[o, g][:, cols, :], w_raw[o, g][:, :, cols].rearrange("p j m -> p m j"))
+                a += n
+
+        def gather(g, u):
+            window = x_pairs[g, u][:].rearrange("p c e -> p (c e)").bitcast(U32)
+            words = x_in[g][:].rearrange("p c k -> p (c k)").bitcast(U32).rearrange("p (c u) -> p c u", u=2)
+            for a, b in GATHERS:
+                nc.vector.tensor_copy(out=words[:, a:b, u], in_=window.indirect(offsets[:, a // 16 : b // 16]))
+
+        def quantize_x(g):
+            for a, b in PIECES:
+                nc.vector.quantize_mx(
+                    out=x_codes[g][:, a:b].bitcast(FP8X4),
+                    scales=x_scales[g][:, a:b],
+                    in_=x_in[g][:, a:b, :].rearrange("p c k -> p (c k)"),
+                )
+
+        def quantize_w(o, g, pieces):
+            for a, b in pieces:
+                nc.vector.quantize_mx(
+                    out=w_codes[o, g][:, a:b].bitcast(FP8X4),
+                    scales=w_scales[o, g][:, a:b],
+                    in_=w_in[o, g][:, a:b, :].rearrange("p c k -> p (c k)"),
+                )
+
+        acc = [psum.tile([P, SITES], F32, name=f"acc{t}") for t in range(2)]
+
+        def multiply(o, g, first, last):
+            sites = slice(o * SITES, (o + 1) * SITES)
+            for t in range(2):
+                chans = slice(t * P, (t + 1) * P)
+                nc.tensor.matmul_mx(
+                    out=acc[t][:],
+                    lhsT=w_codes[o, g][:, chans].bitcast(FP8X4),
+                    lhsT_scale=w_scales[o, g][:, chans],
+                    rhs=x_codes[g][:, sites].bitcast(FP8X4),
+                    rhs_scale=x_scales[g][:, sites],
+                    start=first,
+                    stop=last,
+                )
+
+        cast_x(0, 0, (("s", 512), ("v", 512)))
+        gather(0, 0)
+        cast_x(0, 1, (("s", 1024),))
+        gather(0, 1)
+        cast_x(1, 0, (("s", 1024),))
+        quantize_x(0)
+        gather(1, 0)
+        cast_x(1, 1, (("s", 1024),))
+        gather(1, 1)
+        cast_w(0, 0, (("s", 256),))
+        cast_w(1, 0, (("s", 256),))
+        quantize_x(1)
+        quantize_w(0, 0, ((0, 256),))
+        multiply(0, 0, True, False)
+        cast_w(2, 0, (("v", 256),))
+        quantize_w(1, 0, ((0, 256),))
+        multiply(1, 0, False, False)
+        cast_w(0, 1, (("s", 256),))
+        quantize_w(2, 0, ((0, 256),))
+        multiply(2, 0, False, False)
+        cast_w(1, 1, (("v", 256),))
+        quantize_w(0, 1, ((0, 256),))
+        multiply(0, 1, False, False)
+        cast_w(2, 1, (("v", 128), ("s", 128)))
+        quantize_w(1, 1, ((0, 256),))
+        multiply(1, 1, False, False)
+        quantize_w(2, 1, ((0, 128), (128, 256)))
+        multiply(2, 1, False, True)
+
+        result = [keep.tile([P, SITES], F32, name=f"result{t}") for t in range(2)]
+        nc.vector.tensor_scalar(result[0][:], acc[0][:], bias_t[:, 0:1], None, ADD)
+        nc.sync.dma_start(out=out[0:P, :], in_=result[0][:])
+        nc.scalar.activation(out=result[1][:], in_=acc[1][:], func=IDENTITY, bias=bias_t[:, 1:2])
+        nc.scalar.dma_start(out=out[P : 2 * P, :], in_=result[1][:])

@@ -8,6 +8,7 @@ FLOPS = 2 * RELS * SITES * D * M
 F32 = mybir.dt.float32
 BF16 = mybir.dt.bfloat16
 U32 = mybir.dt.uint32
+I32 = mybir.dt.int32
 U16 = mybir.dt.uint16
 U8 = mybir.dt.uint8
 FP8X4 = mybir.dt.float8_e4m3fn_x4
@@ -41,21 +42,22 @@ def tile_attend_spconv_bias_kernel(tc, xT, w, bias, offs, out):
         for g in range(2):
             for u in range(2):
                 x_raw[g, u] = keep.tile([P, 2, COLS], F32, name=f"x_raw{g}{u}")
-                halves = 2 if (g, u) == (0, 0) else 1
-                step = COLS // halves
-                for h in range(halves):
-                    cols = slice(h * step, (h + 1) * step)
-                    nc.sync.dma_start(out=x_raw[g, u][:, :, cols], in_=x_rows[g, u][:, :, cols])
         w_raw = {}
         for g in range(2):
             for o in range(RELS):
                 w_raw[o, g] = keep.tile([P, 4, M], F32, name=f"w_raw{o}{g}")
-                nc.sync.dma_start(out=w_raw[o, g][:], in_=w_rows[o, g])
 
-        x_pairs, x_in, x_codes, x_scales = {}, {}, {}, {}
+        def load_x(g, u, a, b):
+            nc.sync.dma_start(out=x_raw[g, u][:, :, a:b], in_=x_rows[g, u][:, :, a:b])
+
+        def load_w(o, g):
+            nc.sync.dma_start(out=w_raw[o, g][:], in_=w_rows[o, g])
+
+        x_pairs, gathered, x_in, x_codes, x_scales = {}, {}, {}, {}, {}
         for g in range(2):
             for u in range(2):
                 x_pairs[g, u] = keep.tile([P, COLS, 2], BF16, name=f"x_pairs{g}{u}", align_bytes=64)
+            gathered[g] = keep.tile([P, 2, ENTRIES, 2], BF16, name=f"gathered{g}", align_bytes=64)
             x_in[g] = keep.tile([P, ENTRIES, 4], BF16, name=f"x_in{g}", align_bytes=64)
             x_codes[g] = keep.tile([P, ENTRIES], U32, name=f"x_codes{g}", align_bytes=64)
             x_scales[g] = keep.tile([P, ENTRIES], U8, name=f"x_scales{g}", align_bytes=64)
@@ -67,93 +69,117 @@ def tile_attend_spconv_bias_kernel(tc, xT, w, bias, offs, out):
                 w_scales[o, g] = keep.tile([P, M], U8, name=f"w_scales{o}{g}", align_bytes=64)
 
         def cast(engine, dst, src):
-            if engine == "s":
+            if engine == "S":
                 nc.scalar.activation(out=dst, in_=src, func=COPY)
-            elif engine == "g":
+            elif engine == "G":
                 nc.gpsimd.tensor_scalar(dst, src, 1.0, 0.0, MULT, ADD)
             else:
                 nc.vector.tensor_copy(out=dst, in_=src)
 
-        def cast_x(g, u, parts):
-            a = 0
-            for engine, n in parts:
-                cols = slice(a, a + n)
-                cast(engine, x_pairs[g, u][:, cols, :], x_raw[g, u][:, :, cols].rearrange("p e c -> p c e"))
-                a += n
+        def cast_x(g, u, engine, a, b):
+            cast(engine, x_pairs[g, u][:, a:b, :], x_raw[g, u][:, :, a:b].rearrange("p e c -> p c e"))
 
-        def cast_w(o, g, parts):
-            a = 0
-            for engine, n in parts:
-                cols = slice(a, a + n)
-                cast(engine, w_in[o, g][:, cols, :], w_raw[o, g][:, :, cols].rearrange("p j m -> p m j"))
-                a += n
+        def cast_w(o, g, engine, a, b):
+            cast(engine, w_in[o, g][:, a:b, :], w_raw[o, g][:, :, a:b].rearrange("p j m -> p m j"))
 
-        def gather(g, u):
+        def gather(g, u, a, b):
             window = x_pairs[g, u][:].rearrange("p c e -> p (c e)").bitcast(U32)
-            words = x_in[g][:].rearrange("p c k -> p (c k)").bitcast(U32).rearrange("p (c u) -> p c u", u=2)
-            for a, b in GATHERS:
-                nc.vector.tensor_copy(out=words[:, a:b, u], in_=window.indirect(offsets[:, a // 16 : b // 16]))
+            words = gathered[g][:, u].rearrange("p c e -> p (c e)").bitcast(U32)
+            nc.vector.tensor_copy(out=words[:, a:b], in_=window.indirect(offsets[:, a // 16 : b // 16]))
 
-        def quantize_x(g):
-            for a, b in PIECES:
-                nc.vector.quantize_mx(
-                    out=x_codes[g][:, a:b].bitcast(FP8X4),
-                    scales=x_scales[g][:, a:b],
-                    in_=x_in[g][:, a:b, :].rearrange("p c k -> p (c k)"),
-                )
+        def interleave(g, a, b):
+            src = gathered[g][:].rearrange("p u c e -> p (u c e)").bitcast(I32).rearrange("p (u c) -> p c u", u=2)
+            dst = x_in[g][:].rearrange("p c k -> p (c k)").bitcast(I32).rearrange("p (c u) -> p c u", u=2)
+            nc.vector.tensor_copy(out=dst[:, a:b, :], in_=src[:, a:b, :])
 
-        def quantize_w(o, g, pieces):
-            for a, b in pieces:
-                nc.vector.quantize_mx(
-                    out=w_codes[o, g][:, a:b].bitcast(FP8X4),
-                    scales=w_scales[o, g][:, a:b],
-                    in_=w_in[o, g][:, a:b, :].rearrange("p c k -> p (c k)"),
-                )
+        def quantize_x(g, a, b):
+            nc.vector.quantize_mx(
+                out=x_codes[g][:, a:b].bitcast(FP8X4),
+                scales=x_scales[g][:, a:b],
+                in_=x_in[g][:, a:b, :].rearrange("p c k -> p (c k)"),
+            )
+
+        def quantize_w(o, g, a, b):
+            nc.vector.quantize_mx(
+                out=w_codes[o, g][:, a:b].bitcast(FP8X4),
+                scales=w_scales[o, g][:, a:b],
+                in_=w_in[o, g][:, a:b, :].rearrange("p c k -> p (c k)"),
+            )
 
         acc = [psum.tile([P, SITES], F32, name=f"acc{t}") for t in range(2)]
 
-        def multiply(o, g, first, last):
+        def multiply(o, g, t, first, last):
             sites = slice(o * SITES, (o + 1) * SITES)
-            for t in range(2):
-                chans = slice(t * P, (t + 1) * P)
-                nc.tensor.matmul_mx(
-                    out=acc[t][:],
-                    lhsT=w_codes[o, g][:, chans].bitcast(FP8X4),
-                    lhsT_scale=w_scales[o, g][:, chans],
-                    rhs=x_codes[g][:, sites].bitcast(FP8X4),
-                    rhs_scale=x_scales[g][:, sites],
-                    start=first,
-                    stop=last,
-                )
+            chans = slice(t * P, (t + 1) * P)
+            nc.tensor.matmul_mx(
+                out=acc[t][:],
+                lhsT=w_codes[o, g][:, chans].bitcast(FP8X4),
+                lhsT_scale=w_scales[o, g][:, chans],
+                rhs=x_codes[g][:, sites].bitcast(FP8X4),
+                rhs_scale=x_scales[g][:, sites],
+                start=first,
+                stop=last,
+            )
 
-        cast_x(0, 0, (("s", 512), ("v", 512)))
-        gather(0, 0)
-        cast_x(0, 1, (("s", 1024),))
-        gather(0, 1)
-        cast_x(1, 0, (("s", 1024),))
-        quantize_x(0)
-        gather(1, 0)
-        cast_x(1, 1, (("s", 1024),))
-        gather(1, 1)
-        cast_w(0, 0, (("s", 256),))
-        cast_w(1, 0, (("s", 256),))
-        quantize_x(1)
-        quantize_w(0, 0, ((0, 256),))
-        multiply(0, 0, True, False)
-        cast_w(2, 0, (("v", 256),))
-        quantize_w(1, 0, ((0, 256),))
-        multiply(1, 0, False, False)
-        cast_w(0, 1, (("s", 256),))
-        quantize_w(2, 0, ((0, 256),))
-        multiply(2, 0, False, False)
-        cast_w(1, 1, (("v", 256),))
-        quantize_w(0, 1, ((0, 256),))
-        multiply(0, 1, False, False)
-        cast_w(2, 1, (("v", 128), ("s", 128)))
-        quantize_w(1, 1, ((0, 256),))
-        multiply(1, 1, False, False)
-        quantize_w(2, 1, ((0, 128), (128, 256)))
-        multiply(2, 1, False, True)
+        load_x(0, 0, 0, 512)
+        load_x(0, 0, 512, 1024)
+        load_x(0, 1, 0, 1024)
+        load_x(1, 1, 0, 1024)
+        load_x(1, 0, 0, 1024)
+        load_w(2, 0)
+        load_w(1, 0)
+        load_w(0, 1)
+        load_w(0, 0)
+        load_w(1, 1)
+        load_w(2, 1)
+        cast_x(0, 0, "S", 0, 512)
+        cast_x(0, 0, "V", 512, 1024)
+        gather(0, 0, 0, 384)
+        gather(0, 0, 384, 768)
+        cast_x(0, 1, "S", 0, 512)
+        cast_x(0, 1, "V", 512, 1024)
+        gather(0, 1, 0, 384)
+        gather(0, 1, 384, 768)
+        cast_x(1, 1, "S", 0, 1024)
+        interleave(0, 0, 384)
+        interleave(0, 384, 768)
+        quantize_x(0, 0, 512)
+        cast_x(1, 0, "S", 0, 1024)
+        gather(1, 1, 0, 384)
+        gather(1, 1, 384, 768)
+        cast_w(2, 0, "G", 0, 256)
+        quantize_x(0, 512, 768)
+        gather(1, 0, 0, 384)
+        cast_w(1, 0, "G", 0, 256)
+        gather(1, 0, 384, 768)
+        cast_w(0, 1, "S", 0, 256)
+        quantize_w(2, 0, 0, 256)
+        quantize_w(1, 0, 0, 256)
+        multiply(2, 0, 0, True, False)
+        cast_w(0, 0, "G", 0, 256)
+        interleave(1, 0, 384)
+        multiply(2, 0, 1, True, False)
+        multiply(1, 0, 0, False, False)
+        interleave(1, 384, 768)
+        multiply(1, 0, 1, False, False)
+        quantize_w(0, 1, 0, 256)
+        cast_w(1, 1, "S", 0, 256)
+        quantize_w(0, 0, 0, 256)
+        quantize_x(1, 0, 512)
+        multiply(0, 0, 0, False, False)
+        multiply(0, 0, 1, False, False)
+        quantize_x(1, 512, 768)
+        cast_w(2, 1, "S", 128, 256)
+        multiply(0, 1, 0, False, False)
+        quantize_w(1, 1, 0, 256)
+        multiply(0, 1, 1, False, False)
+        cast_w(2, 1, "V", 0, 128)
+        multiply(1, 1, 0, False, False)
+        multiply(1, 1, 1, False, False)
+        quantize_w(2, 1, 128, 256)
+        quantize_w(2, 1, 0, 128)
+        multiply(2, 1, 1, False, True)
+        multiply(2, 1, 0, False, True)
 
         result = [keep.tile([P, SITES], F32, name=f"result{t}") for t in range(2)]
         nc.vector.tensor_scalar(result[0][:], acc[0][:], bias_t[:, 0:1], None, ADD)

@@ -1,6 +1,7 @@
 from contextlib import ExitStack
 
 import concourse.mybir as mybir
+from concourse.masks import make_identity
 
 RELS, SITES, COLS, D, M = 3, 256, 1024, 1024, 256
 FLOPS = 2 * RELS * SITES * D * M
@@ -30,10 +31,10 @@ def tile_attend_spconv_bias_kernel(tc, xT, w, bias, offs, out):
         psum = ctx.enter_context(tc.psum_pool(name="psum", bufs=1))
 
         offsets = keep.tile([P, ENTRIES // 16], U16, name="offsets")
-        nc.sync.dma_start(offsets[:], offs)
-        bias_t = keep.tile([P, 2], F32, name="bias_t")
-        with nc.allow_non_contiguous_dma(reason="256 biases, one a partition and m tile"):
-            nc.scalar.dma_start(out=bias_t[:], in_=bias.rearrange("(t p) o -> p (t o)", p=P))
+        identity = keep.tile([P, P], F32, name="identity")
+        make_identity(nc, identity[:])
+        bias_rows = keep.tile([P, P], F32, name="bias_rows")
+        nc.gpsimd.memset(bias_rows[:], 0.0)
 
         x_rows = xT.rearrange("(g p u e) c -> g u p e c", g=2, p=P, u=2, e=2)
         w_rows = w.rearrange("o (g p j) m -> o g p j m", g=2, p=P, j=4)
@@ -106,6 +107,8 @@ def tile_attend_spconv_bias_kernel(tc, xT, w, bias, offs, out):
                 in_=w_in[o, g][:, a:b, :].rearrange("p c k -> p (c k)"),
             )
 
+        bias_t = keep.tile([P, 2], F32, name="bias_t")
+        bias_cols = psum.tile([P, P], F32, name="bias_cols")
         acc = [psum.tile([P, SITES], F32, name=f"acc{t}") for t in range(2)]
 
         def multiply(o, g, t, first, last):
@@ -123,15 +126,17 @@ def tile_attend_spconv_bias_kernel(tc, xT, w, bias, offs, out):
 
         load_x(0, 0, 0, 512)
         load_x(0, 0, 512, 1024)
+        nc.sync.dma_start(offsets[:], offs)
         load_x(0, 1, 0, 1024)
-        load_x(1, 1, 0, 1024)
         load_x(1, 0, 0, 1024)
         load_w(2, 0)
+        load_x(1, 1, 0, 1024)
+        load_w(0, 0)
         load_w(1, 0)
         load_w(0, 1)
-        load_w(0, 0)
         load_w(1, 1)
         load_w(2, 1)
+        nc.sync.dma_start(out=bias_rows[0:2, :], in_=bias.rearrange("(t c) o -> t (c o)", t=2))
         cast_x(0, 0, "S", 0, 512)
         cast_x(0, 0, "V", 512, 1024)
         gather(0, 0, 0, 384)
@@ -140,37 +145,42 @@ def tile_attend_spconv_bias_kernel(tc, xT, w, bias, offs, out):
         cast_x(0, 1, "V", 512, 1024)
         gather(0, 1, 0, 384)
         gather(0, 1, 384, 768)
-        cast_x(1, 1, "S", 0, 1024)
+        cast_x(1, 0, "S", 0, 896)
         interleave(0, 0, 384)
         interleave(0, 384, 768)
+        cast_x(1, 0, "V", 896, 1024)
         quantize_x(0, 0, 512)
-        cast_x(1, 0, "S", 0, 1024)
-        gather(1, 1, 0, 384)
-        gather(1, 1, 384, 768)
-        cast_w(2, 0, "G", 0, 256)
+        cast_w(2, 0, "S", 0, 256)
         quantize_x(0, 512, 768)
         gather(1, 0, 0, 384)
-        cast_w(1, 0, "G", 0, 256)
+        cast_x(1, 1, "S", 0, 512)
+        cast_x(1, 1, "V", 512, 1024)
         gather(1, 0, 384, 768)
-        cast_w(0, 1, "S", 0, 256)
+        cast_w(0, 0, "S", 0, 256)
+        gather(1, 1, 0, 384)
+        gather(1, 1, 384, 768)
+        cast_w(1, 0, "S", 0, 256)
         quantize_w(2, 0, 0, 256)
-        quantize_w(1, 0, 0, 256)
-        multiply(2, 0, 0, True, False)
-        cast_w(0, 0, "G", 0, 256)
         interleave(1, 0, 384)
+        multiply(2, 0, 0, True, False)
+        cast_w(0, 1, "S", 0, 192)
         multiply(2, 0, 1, True, False)
-        multiply(1, 0, 0, False, False)
         interleave(1, 384, 768)
-        multiply(1, 0, 1, False, False)
-        quantize_w(0, 1, 0, 256)
-        cast_w(1, 1, "S", 0, 256)
+        nc.tensor.transpose(bias_cols[:], bias_rows[:], identity[:])
+        nc.scalar.activation(out=bias_t[:], in_=bias_cols[:, 0:2], func=COPY)
         quantize_w(0, 0, 0, 256)
-        quantize_x(1, 0, 512)
+        cast_w(0, 1, "V", 192, 256)
         multiply(0, 0, 0, False, False)
+        cast_w(1, 1, "S", 0, 256)
+        quantize_w(1, 0, 0, 256)
         multiply(0, 0, 1, False, False)
+        quantize_w(0, 1, 0, 256)
+        multiply(1, 0, 0, False, False)
+        quantize_x(1, 0, 512)
+        multiply(1, 0, 1, False, False)
         quantize_x(1, 512, 768)
-        cast_w(2, 1, "S", 128, 256)
         multiply(0, 1, 0, False, False)
+        cast_w(2, 1, "S", 128, 256)
         quantize_w(1, 1, 0, 256)
         multiply(0, 1, 1, False, False)
         cast_w(2, 1, "V", 0, 128)

@@ -127,67 +127,68 @@ def tile_attend_spconv_bias_kernel(tc, xT, w, bias, offs, out):
         load_x(0, 0, 0, 512)
         load_x(0, 0, 512, 1024)
         nc.sync.dma_start(offsets[:], offs)
+        nc.sync.dma_start(out=bias_rows[0:2, :], in_=bias.rearrange("(t c) o -> t (c o)", t=2))
         load_x(0, 1, 0, 1024)
         load_x(1, 0, 0, 1024)
-        load_w(2, 0)
         load_x(1, 1, 0, 1024)
         load_w(0, 0)
         load_w(1, 0)
+        load_w(2, 0)
         load_w(0, 1)
         load_w(1, 1)
         load_w(2, 1)
-        nc.sync.dma_start(out=bias_rows[0:2, :], in_=bias.rearrange("(t c) o -> t (c o)", t=2))
         cast_x(0, 0, "S", 0, 512)
-        cast_x(0, 0, "V", 512, 1024)
+        cast_x(0, 0, "V", 512, 768)
+        cast_x(0, 0, "S", 768, 1024)
         gather(0, 0, 0, 384)
         gather(0, 0, 384, 768)
         cast_x(0, 1, "S", 0, 512)
         cast_x(0, 1, "V", 512, 1024)
-        gather(0, 1, 0, 384)
-        gather(0, 1, 384, 768)
-        cast_x(1, 0, "S", 0, 896)
-        interleave(0, 0, 384)
-        interleave(0, 384, 768)
-        cast_x(1, 0, "V", 896, 1024)
-        quantize_x(0, 0, 512)
-        cast_w(2, 0, "S", 0, 256)
-        quantize_x(0, 512, 768)
-        gather(1, 0, 0, 384)
-        cast_x(1, 1, "S", 0, 512)
-        cast_x(1, 1, "V", 512, 1024)
-        gather(1, 0, 384, 768)
-        cast_w(0, 0, "S", 0, 256)
-        gather(1, 1, 0, 384)
-        gather(1, 1, 384, 768)
-        cast_w(1, 0, "S", 0, 256)
-        quantize_w(2, 0, 0, 256)
-        interleave(1, 0, 384)
-        multiply(2, 0, 0, True, False)
-        cast_w(0, 1, "S", 0, 192)
-        multiply(2, 0, 1, True, False)
-        interleave(1, 384, 768)
         nc.tensor.transpose(bias_cols[:], bias_rows[:], identity[:])
         nc.scalar.activation(out=bias_t[:], in_=bias_cols[:, 0:2], func=COPY)
+        gather(0, 1, 0, 384)
+        gather(0, 1, 384, 768)
+        cast_x(1, 0, "S", 0, 1024)
+        interleave(0, 0, 384)
+        interleave(0, 384, 768)
+        quantize_x(0, 0, 512)
+        cast_x(1, 1, "S", 0, 1024)
+        quantize_x(0, 512, 768)
+        gather(1, 0, 0, 384)
+        cast_w(0, 0, "G", 0, 128)
+        gather(1, 0, 384, 768)
+        cast_w(0, 0, "S", 128, 256)
+        cast_w(1, 0, "G", 0, 128)
+        gather(1, 1, 0, 384)
+        cast_w(1, 0, "S", 128, 256)
+        gather(1, 1, 384, 768)
+        cast_w(2, 0, "G", 0, 64)
+        cast_w(2, 0, "S", 64, 256)
         quantize_w(0, 0, 0, 256)
-        cast_w(0, 1, "V", 192, 256)
-        multiply(0, 0, 0, False, False)
-        cast_w(1, 1, "S", 0, 256)
         quantize_w(1, 0, 0, 256)
-        multiply(0, 0, 1, False, False)
-        quantize_w(0, 1, 0, 256)
+        multiply(0, 0, 0, True, False)
+        cast_w(0, 1, "S", 0, 256)
+        interleave(1, 0, 384)
+        multiply(0, 0, 1, True, False)
         multiply(1, 0, 0, False, False)
-        quantize_x(1, 0, 512)
+        interleave(1, 384, 768)
         multiply(1, 0, 1, False, False)
+        quantize_w(2, 0, 0, 256)
+        cast_w(1, 1, "S", 0, 256)
+        quantize_x(1, 0, 512)
+        multiply(2, 0, 0, False, False)
+        multiply(2, 0, 1, False, False)
         quantize_x(1, 512, 768)
-        multiply(0, 1, 0, False, False)
+        quantize_w(0, 1, 0, 256)
         cast_w(2, 1, "S", 128, 256)
         quantize_w(1, 1, 0, 256)
-        multiply(0, 1, 1, False, False)
+        multiply(0, 1, 0, False, False)
         cast_w(2, 1, "V", 0, 128)
+        multiply(0, 1, 1, False, False)
         multiply(1, 1, 0, False, False)
-        multiply(1, 1, 1, False, False)
         quantize_w(2, 1, 128, 256)
         quantize_w(2, 1, 0, 128)
+        multiply(1, 1, 1, False, False)
         multiply(2, 1, 1, False, True)
         multiply(2, 1, 0, False, True)
 

from contextlib import ExitStack

import concourse.mybir as mybir
from concourse.masks import make_identity

RELS, SITES, COLS, D, M = 3, 256, 1024, 1024, 256
FLOPS = 2 * RELS * SITES * D * M

F32 = mybir.dt.float32
BF16 = mybir.dt.bfloat16
U32 = mybir.dt.uint32
I32 = mybir.dt.int32
U16 = mybir.dt.uint16
U8 = mybir.dt.uint8
FP8X4 = mybir.dt.float8_e4m3fn_x4
ADD = mybir.AluOpType.add
MULT = mybir.AluOpType.mult
COPY = mybir.ActivationFunctionType.Copy
IDENTITY = mybir.ActivationFunctionType.Identity

P = 128
ENTRIES = RELS * SITES
GATHERS = ((0, 384), (384, 768))
PIECES = ((0, 512), (512, 768))


def tile_attend_spconv_bias_kernel(tc, xT, w, bias, offs, out):
    nc = tc.nc
    with ExitStack() as ctx:
        keep = ctx.enter_context(tc.tile_pool(name="keep", bufs=1))
        psum = ctx.enter_context(tc.psum_pool(name="psum", bufs=1))

        offsets = keep.tile([P, ENTRIES // 16], U16, name="offsets")
        identity = keep.tile([P, P], F32, name="identity")
        make_identity(nc, identity[:])
        bias_rows = keep.tile([P, P], F32, name="bias_rows")
        nc.gpsimd.memset(bias_rows[:], 0.0)

        x_rows = xT.rearrange("(g p u e) c -> g u p e c", g=2, p=P, u=2, e=2)
        w_rows = w.rearrange("o (g p j) m -> o g p j m", g=2, p=P, j=4)

        x_raw = {}
        for g in range(2):
            for u in range(2):
                x_raw[g, u] = keep.tile([P, 2, COLS], F32, name=f"x_raw{g}{u}")
        w_raw = {}
        for g in range(2):
            for o in range(RELS):
                w_raw[o, g] = keep.tile([P, 4, M], F32, name=f"w_raw{o}{g}")

        def load_x(g, u, a, b):
            nc.sync.dma_start(out=x_raw[g, u][:, :, a:b], in_=x_rows[g, u][:, :, a:b])

        def load_w(o, g):
            nc.sync.dma_start(out=w_raw[o, g][:], in_=w_rows[o, g])

        x_pairs, gathered, x_in, x_codes, x_scales = {}, {}, {}, {}, {}
        for g in range(2):
            for u in range(2):
                x_pairs[g, u] = keep.tile([P, COLS, 2], BF16, name=f"x_pairs{g}{u}", align_bytes=64)
            gathered[g] = keep.tile([P, 2, ENTRIES, 2], BF16, name=f"gathered{g}", align_bytes=64)
            x_in[g] = keep.tile([P, ENTRIES, 4], BF16, name=f"x_in{g}", align_bytes=64)
            x_codes[g] = keep.tile([P, ENTRIES], U32, name=f"x_codes{g}", align_bytes=64)
            x_scales[g] = keep.tile([P, ENTRIES], U8, name=f"x_scales{g}", align_bytes=64)
        w_in, w_codes, w_scales = {}, {}, {}
        for g in range(2):
            for o in range(RELS):
                w_in[o, g] = keep.tile([P, M, 4], BF16, name=f"w_in{o}{g}", align_bytes=64)
                w_codes[o, g] = keep.tile([P, M], U32, name=f"w_codes{o}{g}", align_bytes=64)
                w_scales[o, g] = keep.tile([P, M], U8, name=f"w_scales{o}{g}", align_bytes=64)

        def cast(engine, dst, src):
            if engine == "S":
                nc.scalar.activation(out=dst, in_=src, func=COPY)
            elif engine == "G":
                nc.gpsimd.tensor_scalar(dst, src, 1.0, 0.0, MULT, ADD)
            else:
                nc.vector.tensor_copy(out=dst, in_=src)

        def cast_x(g, u, engine, a, b):
            cast(engine, x_pairs[g, u][:, a:b, :], x_raw[g, u][:, :, a:b].rearrange("p e c -> p c e"))

        def cast_w(o, g, engine, a, b):
            cast(engine, w_in[o, g][:, a:b, :], w_raw[o, g][:, :, a:b].rearrange("p j m -> p m j"))

        def gather(g, u, a, b):
            window = x_pairs[g, u][:].rearrange("p c e -> p (c e)").bitcast(U32)
            words = gathered[g][:, u].rearrange("p c e -> p (c e)").bitcast(U32)
            nc.vector.tensor_copy(out=words[:, a:b], in_=window.indirect(offsets[:, a // 16 : b // 16]))

        def interleave(g, a, b):
            src = gathered[g][:].rearrange("p u c e -> p (u c e)").bitcast(I32).rearrange("p (u c) -> p c u", u=2)
            dst = x_in[g][:].rearrange("p c k -> p (c k)").bitcast(I32).rearrange("p (c u) -> p c u", u=2)
            nc.vector.tensor_copy(out=dst[:, a:b, :], in_=src[:, a:b, :])

        def quantize_x(g, a, b):
            nc.vector.quantize_mx(
                out=x_codes[g][:, a:b].bitcast(FP8X4),
                scales=x_scales[g][:, a:b],
                in_=x_in[g][:, a:b, :].rearrange("p c k -> p (c k)"),
            )

        def quantize_w(o, g, a, b):
            nc.vector.quantize_mx(
                out=w_codes[o, g][:, a:b].bitcast(FP8X4),
                scales=w_scales[o, g][:, a:b],
                in_=w_in[o, g][:, a:b, :].rearrange("p c k -> p (c k)"),
            )

        bias_t = keep.tile([P, 2], F32, name="bias_t")
        bias_cols = psum.tile([P, P], F32, name="bias_cols")
        acc = [psum.tile([P, SITES], F32, name=f"acc{t}") for t in range(2)]

        def multiply(o, g, t, first, last):
            sites = slice(o * SITES, (o + 1) * SITES)
            chans = slice(t * P, (t + 1) * P)
            nc.tensor.matmul_mx(
                out=acc[t][:],
                lhsT=w_codes[o, g][:, chans].bitcast(FP8X4),
                lhsT_scale=w_scales[o, g][:, chans],
                rhs=x_codes[g][:, sites].bitcast(FP8X4),
                rhs_scale=x_scales[g][:, sites],
                start=first,
                stop=last,
            )

        load_x(0, 0, 0, 512)
        load_x(0, 0, 512, 1024)
        nc.sync.dma_start(offsets[:], offs)
        nc.sync.dma_start(out=bias_rows[0:2, :], in_=bias.rearrange("(t c) o -> t (c o)", t=2))
        load_x(0, 1, 0, 1024)
        load_x(1, 0, 0, 1024)
        load_x(1, 1, 0, 1024)
        load_w(0, 0)
        load_w(1, 0)
        load_w(2, 0)
        load_w(0, 1)
        load_w(1, 1)
        load_w(2, 1)
        cast_x(0, 0, "S", 0, 512)
        cast_x(0, 0, "V", 512, 768)
        cast_x(0, 0, "S", 768, 1024)
        gather(0, 0, 0, 384)
        gather(0, 0, 384, 768)
        cast_x(0, 1, "S", 0, 512)
        cast_x(0, 1, "V", 512, 1024)
        nc.tensor.transpose(bias_cols[:], bias_rows[:], identity[:])
        nc.scalar.activation(out=bias_t[:], in_=bias_cols[:, 0:2], func=COPY)
        gather(0, 1, 0, 384)
        gather(0, 1, 384, 768)
        cast_x(1, 0, "S", 0, 1024)
        interleave(0, 0, 384)
        interleave(0, 384, 768)
        quantize_x(0, 0, 512)
        cast_x(1, 1, "S", 0, 1024)
        quantize_x(0, 512, 768)
        gather(1, 0, 0, 384)
        cast_w(0, 0, "G", 0, 128)
        gather(1, 0, 384, 768)
        cast_w(0, 0, "S", 128, 256)
        cast_w(1, 0, "G", 0, 128)
        gather(1, 1, 0, 384)
        cast_w(1, 0, "S", 128, 256)
        gather(1, 1, 384, 768)
        cast_w(2, 0, "G", 0, 64)
        cast_w(2, 0, "S", 64, 256)
        quantize_w(0, 0, 0, 256)
        quantize_w(1, 0, 0, 256)
        multiply(0, 0, 0, True, False)
        cast_w(0, 1, "S", 0, 256)
        interleave(1, 0, 384)
        multiply(0, 0, 1, True, False)
        multiply(1, 0, 0, False, False)
        interleave(1, 384, 768)
        multiply(1, 0, 1, False, False)
        quantize_w(2, 0, 0, 256)
        cast_w(1, 1, "S", 0, 256)
        quantize_x(1, 0, 512)
        multiply(2, 0, 0, False, False)
        multiply(2, 0, 1, False, False)
        quantize_x(1, 512, 768)
        quantize_w(0, 1, 0, 256)
        cast_w(2, 1, "S", 128, 256)
        quantize_w(1, 1, 0, 256)
        multiply(0, 1, 0, False, False)
        cast_w(2, 1, "V", 0, 128)
        multiply(0, 1, 1, False, False)
        multiply(1, 1, 0, False, False)
        quantize_w(2, 1, 128, 256)
        quantize_w(2, 1, 0, 128)
        multiply(1, 1, 1, False, False)
        multiply(2, 1, 1, False, True)
        multiply(2, 1, 0, False, True)

        result = [keep.tile([P, SITES], F32, name=f"result{t}") for t in range(2)]
        nc.vector.tensor_scalar(result[0][:], acc[0][:], bias_t[:, 0:1], None, ADD)
        nc.sync.dma_start(out=out[0:P, :], in_=result[0][:])
        nc.scalar.activation(out=result[1][:], in_=acc[1][:], func=IDENTITY, bias=bias_t[:, 1:2])
        nc.scalar.dma_start(out=out[P : 2 * P, :], in_=result[1][:])
